import numpy as np
import ml_dtypes


def mxq(x, axis, fmt="e4m3"):
    dtype, down = {"e4m3": (ml_dtypes.float8_e4m3fn, 7), "e5m2": (ml_dtypes.float8_e5m2, 14)}[fmt]
    v = np.moveaxis(np.asarray(x, np.float32).astype(ml_dtypes.bfloat16).astype(np.float64), axis, -1)
    blocks = v.reshape(v.shape[:-1] + (-1, 32))
    amax = np.abs(blocks).max(-1, keepdims=True)
    byte = np.maximum(np.where(amax > 0, np.frexp(amax)[1] - 1 + 127, 0) - down, 1)
    scale = np.exp2(byte - 127.0)
    codes = (blocks / scale).astype(np.float32).astype(dtype).astype(np.float64)
    return np.moveaxis((codes * scale).reshape(v.shape), -1, axis)


WIDE = False


def mx_kscale(k):
    if not WIDE:
        return np.ones(k)
    levels = np.array([10, -10, 5, -5, 0])
    if k % 512:
        return np.exp2(np.random.permutation(np.resize(levels, k // 32))).repeat(32)
    a = np.empty((k // 512, 16))
    for p in range(k // 512):
        a[p, :8] = np.random.permutation(np.resize(levels, 8))
        for g in range(8):
            far = levels[np.abs(levels - a[p, g]) >= 10]
            a[p, g + 8] = far[np.random.randint(len(far))]
    return np.exp2(a.ravel()).repeat(32)


BF16 = ml_dtypes.bfloat16


def bf(x):
    return np.asarray(x, np.float32).astype(BF16)


def f64(x):
    return np.asarray(x).astype(np.float64)


E2M1 = np.array([0.0, 0.5, 1.0, 1.5, 2.0, 3.0, 4.0, 6.0, -0.0, -0.5, -1.0, -1.5, -2.0, -3.0, -4.0, -6.0])


def pack_weight(w, fmt):
    k, n = w.shape
    w = f64(bf(w)).reshape(k // 32, 32, n)
    amax = np.abs(w).max(1)
    if fmt == "e4m3":
        byte = np.frexp(amax)[1] - 1 + 127 - 7
    else:
        mant, ex = np.frexp(amax / 6.0)
        byte = np.where(mant > 0.5, ex, ex - 1) + 127
    byte = np.clip(np.where(amax > 0, byte, 1), 1, 254)
    scaled = (w * np.exp2(127.0 - byte)[:, None, :]).reshape(k, n).astype(np.float32)
    by_word = np.ascontiguousarray(scaled.reshape(k // 512, 128, 4, n).transpose(0, 1, 3, 2))
    if fmt == "e4m3":
        words = by_word.astype(ml_dtypes.float8_e4m3fn).view(np.uint8)
    else:
        c = by_word.astype(ml_dtypes.float4_e2m1fn).view(np.uint8) & 0xF
        words = c[..., 0::2] | (c[..., 1::2] << 4)
    return np.ascontiguousarray(words), np.ascontiguousarray(byte.astype(np.uint8).reshape(k // 512, 16, n))


def unpack_weight(words, scales, fmt):
    g, p, n, _ = words.shape
    if fmt == "e4m3":
        vals = np.ascontiguousarray(words).view(ml_dtypes.float8_e4m3fn).astype(np.float64)
    else:
        nib = np.empty((g, p, n, 4), np.uint8)
        nib[..., 0::2] = words & 0xF
        nib[..., 1::2] = words >> 4
        vals = E2M1[nib]
    vals = vals * np.repeat(np.exp2(scales.astype(np.float64) - 127.0), 8, axis=1)[..., None]
    return vals.transpose(0, 1, 3, 2).reshape(g * 512, n)
def pack4(w):
    words, scales = pack_weight(w, "e2m1")
    return words.reshape(words.shape[0], 128, -1), scales


def unpack4(words, scales):
    return unpack_weight(words.reshape(words.shape[0], 128, -1, 2), scales, "e2m1")


M, K, F, P, N = 1024, 2048, 1024, 1536, 1024


def setup_inputs():
    s = mx_kscale(K)
    r = mx_kscale(P)
    u = mx_kscale(M)
    a = np.random.standard_normal((K, M)) * s[:, None] * u
    v = np.random.standard_normal((K, F)) / np.sqrt(K) / s[:, None]
    a_words, a_scales = pack4(a)
    v_words, v_scales = pack4(v)
    err = np.random.standard_normal((M, P)) / M ** 0.25 * r / u[:, None]
    w_next = np.random.standard_normal((P, N)) / np.sqrt(P) / r[:, None]
    neg_w = -0.3 * np.random.standard_normal((F, N))
    return {"a_words": a_words, "a_scales": a_scales,
            "v_words": v_words, "v_scales": v_scales,
            "err": bf(err), "w_next": bf(w_next), "neg_w": bf(neg_w)}


def reference(a_words, a_scales, v_words, v_scales, err, w_next, neg_w):
    a = unpack4(a_words, a_scales)
    v = unpack4(v_words, v_scales)
    x = np.maximum(a.T @ v, 0.0)
    d = mxq(f64(err), 1, "e4m3") @ mxq(f64(w_next), 0, "e4m3")
    grad = mxq(x, 0, "e4m3").T @ mxq(d, 0, "e4m3")
    scores = grad * f64(neg_w)
    mask = 1.0 / (1.0 + np.exp(-scores))
    return scores, mask

@@ -1,0 +1,335 @@
+from contextlib import ExitStack
+
+import concourse.mybir as mybir
+from concourse.masks import make_identity
+
+M, K, F, P, N = 1024, 2048, 1024, 1536, 1024
+FLOPS = 2 * M * K * F + 2 * M * P * N + 2 * M * F * N
+
+F32 = mybir.dt.float32
+BF16 = mybir.dt.bfloat16
+I32 = mybir.dt.int32
+U32 = mybir.dt.uint32
+U8 = mybir.dt.uint8
+FP8X4 = mybir.dt.float8_e4m3fn_x4
+FP4X4 = mybir.dt.float4_e2m1fn_x4
+ACT = mybir.ActivationFunctionType
+ALU = mybir.AluOpType
+
+PARTS = 128
+PASS = 512
+BANK = 512
+BANKS = 8
+K_PASSES = K // PASS
+P_PASSES = P // PASS
+GROUPS = M // PASS
+WIDE = 256
+NARROW = 128
+OUT_BUFS = 8
+
+
+def tile_movement_pruning_scores_s12_kernel(
+    tc, a_words, a_scales, v_words, v_scales, err, w_next, neg_w, out_0, out_1
+):
+    nc = tc.nc
+    with ExitStack() as ctx:
+        keep = ctx.enter_context(tc.tile_pool(name="keep", bufs=1))
+        stage = ctx.enter_context(tc.tile_pool(name="stage", bufs=3))
+        outs = ctx.enter_context(tc.tile_pool(name="outs", bufs=OUT_BUFS))
+        psum = ctx.enter_context(tc.psum_pool(name="psum", bufs=1))
+        ctx.enter_context(tc.manual_schedule())
+
+        def kept(name, shape, dtype):
+            return keep.tile(shape, dtype, name=name, align_bytes=64)
+
+        banks_taken = []
+
+        def take_bank():
+            name = "bank%d" % (len(banks_taken) % BANKS)
+            banks_taken.append(name)
+            return psum.tile([PARTS, BANK], F32, name=name)
+
+        a_raw = [kept("a_raw%d" % g, [PARTS, K_PASSES, 2 * PASS], U8) for g in range(GROUPS)]
+        a_codes = [kept("a_codes%d" % g, [PARTS, K_PASSES, 2 * PASS], U8) for g in range(GROUPS)]
+        a_scale_raw = [kept("a_scale_raw%d" % g, [PARTS, K_PASSES, PASS], U8) for g in range(GROUPS)]
+        a_scale = [kept("a_scale%d" % g, [PARTS, K_PASSES, PASS], U8) for g in range(GROUPS)]
+        v_spans = [(0, WIDE), (WIDE, 2 * WIDE), (2 * WIDE, F)]
+        v_codes = [kept("v_codes%d" % lo, [PARTS, K_PASSES, 2 * (hi - lo)], U8) for lo, hi in v_spans]
+        v_scale = [kept("v_scale%d" % h, [PARTS, K_PASSES, BANK], U8) for h in range(2)]
+        err_raw = {(g, h): kept("err_raw%d%d" % (g, h), [PARTS, 2, P], BF16) for g in range(GROUPS) for h in range(2)}
+        err_bf = {(g, s): kept("err_bf%d%d" % (g, s), [PARTS, 4 * PASS], BF16) for g in range(GROUPS) for s in range(P_PASSES)}
+        err_codes = {key: kept("err_codes%d%d" % key, [PARTS, PASS], U32) for key in err_bf}
+        err_scale = {key: kept("err_scale%d%d" % key, [PARTS, PASS], U8) for key in err_bf}
+        w_raw = {(s, h): kept("w_raw%d%d" % (s, h), [PARTS, 4, BANK], BF16) for s in range(P_PASSES) for h in range(2)}
+        w_codes = {key: kept("w_codes%d%d" % key, [PARTS, BANK], U32) for key in w_raw}
+        w_scale = {key: kept("w_scale%d%d" % key, [PARTS, BANK], U8) for key in w_raw}
+        x_codes = [kept("x_codes%d" % g, [PARTS, F], U32) for g in range(GROUPS)]
+        x_scale = [kept("x_scale%d" % g, [PARTS, F], U8) for g in range(GROUPS)]
+        d_codes = [kept("d_codes%d" % g, [PARTS, N], U32) for g in range(GROUPS)]
+        d_scale = [kept("d_scale%d" % g, [PARTS, N], U8) for g in range(GROUPS)]
+        neg_w_sb = [kept("neg_w%d" % h, [PARTS, 4, N], BF16) for h in range(2)]
+        ident = kept("ident", [PARTS, PARTS], F32)
+
+        for plane in (a_scale_raw[0], v_scale[0], a_scale_raw[1], v_scale[1]):
+            nc.vector.memset(plane[:].bitcast(I32), 0)
+        make_identity(nc, ident[:])
+
+        def load_codes(tile, words, lo, hi):
+            src = words.bitcast(I32).rearrange("s p w -> p s w")
+            nc.sync.dma_start(out=tile[:].bitcast(I32), in_=src[:, :, lo // 2 : hi // 2])
+
+        def load_scales(plane, rows, lo):
+            src = rows.bitcast(I32).rearrange("s (quad r) w -> r quad s w", r=4)
+            for r in range(4):
+                nc.sync.dma_start(
+                    out=plane[r:PARTS:32, :, :].bitcast(I32), in_=src[r][:, :, lo // 4 : (lo + PASS) // 4]
+                )
+
+        def load_err(g, h):
+            rows = err[PASS * g + 256 * h : PASS * g + 256 * (h + 1), :]
+            nc.sync.dma_start(out=err_raw[g, h][:], in_=rows.rearrange("(j p) k -> p j k", p=PARTS))
+
+        def load_w(s, h):
+            rows = w_next[PASS * s : PASS * (s + 1), BANK * h : BANK * (h + 1)]
+            nc.sync.dma_start(out=w_raw[s, h][:], in_=rows.rearrange("(p j) n -> p j n", j=4))
+
+        def load_neg_w(h):
+            rows = neg_w[PASS * h : PASS * (h + 1), :]
+            nc.sync.dma_start(out=neg_w_sb[h][:], in_=rows.rearrange("(j p) n -> p j n", p=PARTS))
+
+        load_codes(a_raw[0], a_words, 0, PASS)
+        load_codes(v_codes[0], v_words, *v_spans[0])
+        load_scales(a_scale_raw[0], a_scales, 0)
+        load_scales(v_scale[0], v_scales, 0)
+        load_codes(v_codes[1], v_words, *v_spans[1])
+        load_err(0, 0)
+        load_codes(a_raw[1], a_words, PASS, 2 * PASS)
+        load_scales(a_scale_raw[1], a_scales, PASS)
+        load_err(0, 1)
+        for s in range(P_PASSES):
+            load_w(s, 0)
+        load_err(1, 0)
+        load_err(1, 1)
+        for s in range(P_PASSES):
+            load_w(s, 1)
+        load_neg_w(0)
+        load_codes(v_codes[2], v_words, *v_spans[2])
+        load_scales(v_scale[1], v_scales, BANK)
+        load_neg_w(1)
+
+        def deal(dst, src, run):
+            nc.vector.tensor_copy(
+                out=dst[:].bitcast(I32).rearrange("p s (t q w) -> p s t q w", t=4, w=run),
+                in_=src[:].bitcast(I32).rearrange("p s (q t w) -> p s t q w", t=4, w=run),
+            )
+
+        def deal_a_codes(g):
+            deal(a_codes[g], a_raw[g], 4)
+
+        def deal_a_scales(g):
+            deal(a_scale[g], a_scale_raw[g], 2)
+
+        def quantize(codes, scale, values):
+            nc.vector.quantize_mx(out=codes.bitcast(FP8X4), scales=scale, in_=values)
+
+        def transpose_err(g, h):
+            words = err_raw[g, h][:].bitcast(F32)
+            for s in range(P_PASSES):
+                bank = take_bank()
+                for j in range(2):
+                    for u in range(2):
+                        nc.tensor.transpose(
+                            bank[:, 256 * u + 128 * j : 256 * u + 128 * (j + 1)],
+                            words[:, j, 256 * s + u : 256 * (s + 1) : 2],
+                            ident[:],
+                        )
+                dst = err_bf[g, s][:].bitcast(F32).rearrange("p (t q r u) -> p t q r u", t=4, r=8, u=2)
+                nc.scalar.copy(
+                    out=dst[:, :, 8 * h : 8 * (h + 1), :, :],
+                    in_=bank[:].rearrange("p (u q t r) -> p t q r u", u=2, t=4, r=8),
+                )
+
+        def quantize_err(g, s):
+            quantize(err_codes[g, s][:], err_scale[g, s][:], err_bf[g, s][:])
+
+        def interleave_w(s, h):
+            w_bf = stage.tile([PARTS, 4 * BANK], BF16, name="w_bf", align_bytes=64)
+            nc.vector.tensor_copy(
+                out=w_bf[:].rearrange("p (c i j) -> p c j i", i=4, j=4),
+                in_=w_raw[s, h][:].rearrange("p j (c i) -> p c j i", i=4),
+            )
+            return lambda: quantize(w_codes[s, h][:], w_scale[s, h][:], w_bf[:])
+
+        def token_product(passes, operands, width, evacuate, codes, scale):
+            slots = BANK // width
+            values = stage.tile([PARTS, 4 * WIDE], BF16, name="values", align_bytes=64)
+            staged = values
+            if slots < 4:
+                staged = stage.tile([PARTS, 4 * WIDE], BF16, name="pairs", align_bytes=64)
+            for b in range(4 // slots):
+                bank = take_bank()
+                for e in range(slots):
+                    for s in range(passes):
+                        lhs, lhs_scale, rhs, rhs_scale = operands(s, slots * b + e)
+                        nc.tensor.matmul_mx(
+                            out=bank[:, width * e : width * (e + 1)],
+                            lhsT=lhs,
+                            lhsT_scale=lhs_scale,
+                            rhs=rhs,
+                            rhs_scale=rhs_scale,
+                            start=(s == 0),
+                            stop=(s == passes - 1),
+                        )
+                evacuate(
+                    staged[:, BANK * b : BANK * (b + 1)].rearrange("p (n e) -> p n e", e=slots),
+                    bank[:].rearrange("p (e n) -> p n e", e=slots),
+                )
+
+            def join_pairs():
+                nc.vector.tensor_copy(
+                    out=values[:].bitcast(I32).rearrange("p (n b) -> p n b", b=2),
+                    in_=staged[:].bitcast(I32).rearrange("p (b n) -> p n b", b=2),
+                )
+
+            return join_pairs, lambda: quantize(codes, scale, values[:, : 4 * width])
+
+        def x_product(g, f0, width):
+            span = max(i for i, (lo, hi) in enumerate(v_spans) if lo <= f0)
+            c0 = f0 - v_spans[span][0]
+            h, s0 = divmod(f0, BANK)
+
+            def operands(s, t):
+                return (
+                    a_codes[g][:, s, 256 * t : 256 * (t + 1)].bitcast(FP4X4),
+                    a_scale[g][:, s, 128 * t : 128 * (t + 1)],
+                    v_codes[span][:, s, 2 * c0 : 2 * (c0 + width)].bitcast(FP4X4),
+                    v_scale[h][:, s, s0 : s0 + width],
+                )
+
+            def evacuate(dst, src):
+                nc.scalar.activation(out=dst, in_=src, func=ACT.Relu)
+
+            cols = slice(f0, f0 + width)
+            return token_product(K_PASSES, operands, width, evacuate, x_codes[g][:, cols], x_scale[g][:, cols])
+
+        def d_product(g, n0):
+            h, c0 = divmod(n0, BANK)
+
+            def operands(s, t):
+                return (
+                    err_codes[g, s][:, 128 * t : 128 * (t + 1)].bitcast(FP8X4),
+                    err_scale[g, s][:, 128 * t : 128 * (t + 1)],
+                    w_codes[s, h][:, c0 : c0 + WIDE].bitcast(FP8X4),
+                    w_scale[s, h][:, c0 : c0 + WIDE],
+                )
+
+            def evacuate(dst, src):
+                nc.scalar.copy(out=dst, in_=src)
+
+            cols = slice(n0, n0 + WIDE)
+            return token_product(P_PASSES, operands, WIDE, evacuate, d_codes[g][:, cols], d_scale[g][:, cols])
+
+        def grad_tile(ft, h):
+            rows = slice(PARTS * ft, PARTS * (ft + 1))
+            cols = slice(BANK * h, BANK * (h + 1))
+            bank = take_bank()
+            for g in range(GROUPS):
+                nc.tensor.matmul_mx(
+                    out=bank[:],
+                    lhsT=x_codes[g][:, rows].bitcast(FP8X4),
+                    lhsT_scale=x_scale[g][:, rows],
+                    rhs=d_codes[g][:, cols].bitcast(FP8X4),
+                    rhs_scale=d_scale[g][:, cols],
+                    start=(g == 0),
+                    stop=(g == GROUPS - 1),
+                )
+            scores = outs.tile([PARTS, BANK], F32, name="scores")
+            nc.vector.tensor_tensor(out=scores[:], in0=bank[:], in1=neg_w_sb[ft // 4][:, ft % 4, cols], op=ALU.mult)
+            nc.sync.dma_start(out=out_0[rows, cols], in_=scores[:])
+            mask = outs.tile([PARTS, BANK], F32, name="mask")
+            nc.scalar.activation(out=mask[:], in_=scores[:], func=ACT.Sigmoid)
+            nc.sync.dma_start(out=out_1[rows, cols], in_=mask[:])
+
+        deal_a_codes(0)
+        deal_a_scales(0)
+        join, quant = x_product(0, 0, WIDE)
+        join_b, quant_b = x_product(0, WIDE, WIDE)
+        join()
+        deal_a_codes(1)
+        quant()
+        deal_a_scales(1)
+        transpose_err(0, 0)
+        join_b()
+        join, quant = x_product(1, 0, WIDE)
+        quant_w = interleave_w(0, 0)
+        quant_b()
+        quant_w()
+        transpose_err(0, 1)
+        quant_w = interleave_w(1, 0)
+        join()
+        quant_w()
+        quant()
+        quant_w = interleave_w(2, 0)
+        join, quant = x_product(1, WIDE, WIDE)
+        quantize_err(0, 0)
+        quant_w()
+        quantize_err(0, 1)
+        quantize_err(0, 2)
+        transpose_err(1, 0)
+        join()
+        quant_w = interleave_w(0, 1)
+        quant()
+        quant_w()
+        join, quant = d_product(0, 0)
+        transpose_err(1, 1)
+        quant_w = interleave_w(1, 1)
+        join()
+        quant_w()
+        quant()
+        for s in range(P_PASSES):
+            quantize_err(1, s)
+        join, quant = d_product(0, WIDE)
+        join_b, quant_b = d_product(1, 0)
+        quant_w = interleave_w(2, 1)
+        join()
+        quant_w()
+        quant()
+        join, quant = d_product(1, WIDE)
+        join_b()
+        quant_b()
+        join_b, quant_b = d_product(0, 2 * WIDE)
+        join()
+        quant()
+
+        def two_grads(first, second, join, quant):
+            grad_tile(*first)
+            join()
+            grad_tile(*second)
+            quant()
+
+        two_grads((0, 0), (1, 0), join_b, quant_b)
+        two_grads((2, 0), (3, 0), *d_product(1, 2 * WIDE))
+        join, quant = d_product(0, 3 * WIDE)
+        join_b, quant_b = d_product(1, 3 * WIDE)
+        join()
+        quant()
+        join, quant = x_product(0, 2 * WIDE, WIDE)
+        join_b()
+        quant_b()
+        two_grads((0, 1), (1, 1), join, quant)
+        two_grads((2, 1), (3, 1), *x_product(1, 2 * WIDE, WIDE))
+        quant = x_product(0, 6 * NARROW, NARROW)[1]
+        grad_tile(4, 0)
+        quant()
+        quant = x_product(1, 6 * NARROW, NARROW)[1]
+        grad_tile(4, 1)
+        quant()
+        grad_tile(5, 0)
+        quant = x_product(0, 7 * NARROW, NARROW)[1]
+        grad_tile(5, 1)
+        quant()
+        quant = x_product(1, 7 * NARROW, NARROW)[1]
+        quant()
+        for ft in (6, 7):
+            for h in range(2):
+                grad_tile(ft, h)

@@ -73,14 +73,16 @@ def tile_movement_pruning_scores_s12_kernel(
         for plane in (a_scale_raw[0], v_scale[0], a_scale_raw[1], v_scale[1]):
             nc.vector.memset(plane[:].bitcast(I32), 0)
         make_identity(nc, ident[:])
+        warm = kept("warm", [PARTS, 8], F32)
+        nc.scalar.activation(out=warm[:], in_=ident[:, 0:8], func=ACT.Sigmoid)
 
         def load_codes(tile, words, lo, hi):
             src = words.bitcast(I32).rearrange("s p w -> p s w")
             nc.sync.dma_start(out=tile[:].bitcast(I32), in_=src[:, :, lo // 2 : hi // 2])
 
-        def load_scales(plane, rows, lo):
+        def load_scales(plane, rows, lo, residues=range(4)):
             src = rows.bitcast(I32).rearrange("s (quad r) w -> r quad s w", r=4)
-            for r in range(4):
+            for r in residues:
                 nc.sync.dma_start(
                     out=plane[r:PARTS:32, :, :].bitcast(I32), in_=src[r][:, :, lo // 4 : (lo + PASS) // 4]
                 )
@@ -97,21 +99,24 @@ def tile_movement_pruning_scores_s12_kernel(
             rows = neg_w[PASS * h : PASS * (h + 1), :]
             nc.sync.dma_start(out=neg_w_sb[h][:], in_=rows.rearrange("(j p) n -> p j n", p=PARTS))
 
-        load_codes(a_raw[0], a_words, 0, PASS)
         load_codes(v_codes[0], v_words, *v_spans[0])
-        load_scales(a_scale_raw[0], a_scales, 0)
+        load_scales(a_scale_raw[0], a_scales, 0, (0, 1))
+        load_codes(a_raw[0], a_words, 0, PASS)
+        load_scales(a_scale_raw[0], a_scales, 0, (2, 3))
         load_scales(v_scale[0], v_scales, 0)
         load_codes(v_codes[1], v_words, *v_spans[1])
+        load_w(0, 0)
         load_err(0, 0)
         load_codes(a_raw[1], a_words, PASS, 2 * PASS)
         load_scales(a_scale_raw[1], a_scales, PASS)
         load_err(0, 1)
-        for s in range(P_PASSES):
-            load_w(s, 0)
+        load_w(1, 0)
+        load_w(2, 0)
         load_err(1, 0)
+        load_w(0, 1)
         load_err(1, 1)
-        for s in range(P_PASSES):
-            load_w(s, 1)
+        load_w(1, 1)
+        load_w(2, 1)
         load_neg_w(0)
         load_codes(v_codes[2], v_words, *v_spans[2])
         load_scales(v_scale[1], v_scales, BANK)
@@ -229,20 +234,30 @@ def tile_movement_pruning_scores_s12_kernel(
             cols = slice(n0, n0 + WIDE)
             return token_product(P_PASSES, operands, WIDE, evacuate, d_codes[g][:, cols], d_scale[g][:, cols])
 
-        def grad_tile(ft, h):
+        def grad_pass(ft, h, g, bank):
             rows = slice(PARTS * ft, PARTS * (ft + 1))
             cols = slice(BANK * h, BANK * (h + 1))
+            nc.tensor.matmul_mx(
+                out=bank[:],
+                lhsT=x_codes[g][:, rows].bitcast(FP8X4),
+                lhsT_scale=x_scale[g][:, rows],
+                rhs=d_codes[g][:, cols].bitcast(FP8X4),
+                rhs_scale=d_scale[g][:, cols],
+                start=(g == 0),
+                stop=(g == GROUPS - 1),
+            )
+
+        def open_grad(ft, h):
             bank = take_bank()
-            for g in range(GROUPS):
-                nc.tensor.matmul_mx(
-                    out=bank[:],
-                    lhsT=x_codes[g][:, rows].bitcast(FP8X4),
-                    lhsT_scale=x_scale[g][:, rows],
-                    rhs=d_codes[g][:, cols].bitcast(FP8X4),
-                    rhs_scale=d_scale[g][:, cols],
-                    start=(g == 0),
-                    stop=(g == GROUPS - 1),
-                )
+            grad_pass(ft, h, 0, bank)
+            return bank
+
+        def grad_tile(ft, h, bank=None):
+            rows = slice(PARTS * ft, PARTS * (ft + 1))
+            cols = slice(BANK * h, BANK * (h + 1))
+            if bank is None:
+                bank = open_grad(ft, h)
+            grad_pass(ft, h, 1, bank)
             scores = outs.tile([PARTS, BANK], F32, name="scores")
             nc.vector.tensor_tensor(out=scores[:], in0=bank[:], in1=neg_w_sb[ft // 4][:, ft % 4, cols], op=ALU.mult)
             nc.sync.dma_start(out=out_0[rows, cols], in_=scores[:])
@@ -253,6 +268,7 @@ def tile_movement_pruning_scores_s12_kernel(
         deal_a_codes(0)
         deal_a_scales(0)
         join, quant = x_product(0, 0, WIDE)
+        interleave_w(0, 0)()
         join_b, quant_b = x_product(0, WIDE, WIDE)
         join()
         deal_a_codes(1)
@@ -261,20 +277,17 @@ def tile_movement_pruning_scores_s12_kernel(
         transpose_err(0, 0)
         join_b()
         join, quant = x_product(1, 0, WIDE)
-        quant_w = interleave_w(0, 0)
+        quant_w = interleave_w(1, 0)
         quant_b()
         quant_w()
         transpose_err(0, 1)
-        quant_w = interleave_w(1, 0)
         join()
-        quant_w()
-        quant()
         quant_w = interleave_w(2, 0)
-        join, quant = x_product(1, WIDE, WIDE)
-        quantize_err(0, 0)
+        quant()
         quant_w()
-        quantize_err(0, 1)
-        quantize_err(0, 2)
+        join, quant = x_product(1, WIDE, WIDE)
+        for s in range(P_PASSES):
+            quantize_err(0, s)
         transpose_err(1, 0)
         join()
         quant_w = interleave_w(0, 1)
@@ -285,9 +298,9 @@ def tile_movement_pruning_scores_s12_kernel(
         quant_w = interleave_w(1, 1)
         join()
         quant_w()
-        quant()
         for s in range(P_PASSES):
             quantize_err(1, s)
+        quant()
         join, quant = d_product(0, WIDE)
         join_b, quant_b = d_product(1, 0)
         quant_w = interleave_w(2, 1)
@@ -307,15 +320,19 @@ def tile_movement_pruning_scores_s12_kernel(
             grad_tile(*second)
             quant()
 
+        join, quant = d_product(1, 2 * WIDE)
         two_grads((0, 0), (1, 0), join_b, quant_b)
-        two_grads((2, 0), (3, 0), *d_product(1, 2 * WIDE))
-        join, quant = d_product(0, 3 * WIDE)
-        join_b, quant_b = d_product(1, 3 * WIDE)
+        join_b, quant_b = d_product(0, 3 * WIDE)
         join()
         quant()
-        join, quant = x_product(0, 2 * WIDE, WIDE)
+        join, quant = d_product(1, 3 * WIDE)
         join_b()
         quant_b()
+        join()
+        grad_tile(2, 0)
+        quant()
+        grad_tile(3, 0)
+        join, quant = x_product(0, 2 * WIDE, WIDE)
         two_grads((0, 1), (1, 1), join, quant)
         two_grads((2, 1), (3, 1), *x_product(1, 2 * WIDE, WIDE))
         quant = x_product(0, 6 * NARROW, NARROW)[1]
@@ -328,8 +345,10 @@ def tile_movement_pruning_scores_s12_kernel(
         quant = x_product(0, 7 * NARROW, NARROW)[1]
         grad_tile(5, 1)
         quant()
+        grad_tile(6, 0)
         quant = x_product(1, 7 * NARROW, NARROW)[1]
         quant()
-        for ft in (6, 7):
-            for h in range(2):
-                grad_tile(ft, h)
+        grad_tile(6, 1)
+        opened = [open_grad(7, h) for h in range(2)]
+        for h in range(2):
+            grad_tile(7, h, opened[h])

@@ -109,13 +109,13 @@ def tile_movement_pruning_scores_s12_kernel(
         load_err(0, 0)
         load_codes(a_raw[1], a_words, PASS, 2 * PASS)
         load_scales(a_scale_raw[1], a_scales, PASS)
-        load_err(0, 1)
         load_w(1, 0)
+        load_err(0, 1)
         load_w(2, 0)
         load_err(1, 0)
         load_w(0, 1)
-        load_err(1, 1)
         load_w(1, 1)
+        load_err(1, 1)
         load_w(2, 1)
         load_neg_w(0)
         load_codes(v_codes[2], v_words, *v_spans[2])
@@ -212,7 +212,10 @@ def tile_movement_pruning_scores_s12_kernel(
                 )
 
             def evacuate(dst, src):
-                nc.scalar.activation(out=dst, in_=src, func=ACT.Relu)
+                if width == NARROW:
+                    nc.vector.tensor_scalar(out=dst, in0=src, scalar1=0.0, scalar2=None, op0=ALU.max)
+                else:
+                    nc.scalar.activation(out=dst, in_=src, func=ACT.Relu)
 
             cols = slice(f0, f0 + width)
             return token_product(K_PASSES, operands, width, evacuate, x_codes[g][:, cols], x_scale[g][:, cols])
@@ -275,35 +278,35 @@ def tile_movement_pruning_scores_s12_kernel(
         quant()
         deal_a_scales(1)
         transpose_err(0, 0)
-        join_b()
         join, quant = x_product(1, 0, WIDE)
         quant_w = interleave_w(1, 0)
+        join_b()
+        quant_w()
         quant_b()
-        quant_w()
         transpose_err(0, 1)
-        join()
         quant_w = interleave_w(2, 0)
-        quant()
+        join()
         quant_w()
+        quant()
         join, quant = x_product(1, WIDE, WIDE)
         for s in range(P_PASSES):
             quantize_err(0, s)
         transpose_err(1, 0)
-        join()
         quant_w = interleave_w(0, 1)
-        quant()
+        join()
         quant_w()
+        quant()
         join, quant = d_product(0, 0)
         transpose_err(1, 1)
-        quant_w = interleave_w(1, 1)
-        join()
-        quant_w()
+        interleave_w(1, 1)()
         for s in range(P_PASSES):
             quantize_err(1, s)
-        quant()
+        join()
+        quant_first = quant
         join, quant = d_product(0, WIDE)
         join_b, quant_b = d_product(1, 0)
         quant_w = interleave_w(2, 1)
+        quant_first()
         join()
         quant_w()
         quant()
@@ -334,7 +337,11 @@ def tile_movement_pruning_scores_s12_kernel(
         grad_tile(3, 0)
         join, quant = x_product(0, 2 * WIDE, WIDE)
         two_grads((0, 1), (1, 1), join, quant)
-        two_grads((2, 1), (3, 1), *x_product(1, 2 * WIDE, WIDE))
+        join, quant = x_product(1, 2 * WIDE, WIDE)
+        join()
+        grad_tile(2, 1)
+        quant()
+        grad_tile(3, 1)
         quant = x_product(0, 6 * NARROW, NARROW)[1]
         grad_tile(4, 0)
         quant()

@@ -25,7 +25,7 @@ P_PASSES = P // PASS
 GROUPS = M // PASS
 WIDE = 256
 NARROW = 128
-OUT_BUFS = 8
+OUT_BUFS = 6
 
 
 def tile_movement_pruning_scores_s12_kernel(
@@ -42,6 +42,7 @@ def tile_movement_pruning_scores_s12_kernel(
         def kept(name, shape, dtype):
             return keep.tile(shape, dtype, name=name, align_bytes=64)
 
+        err_sorted = {}
         banks_taken = []
 
         def take_bank():
@@ -104,18 +105,18 @@ def tile_movement_pruning_scores_s12_kernel(
         load_codes(a_raw[0], a_words, 0, PASS)
         load_scales(a_scale_raw[0], a_scales, 0, (2, 3))
         load_scales(v_scale[0], v_scales, 0)
-        load_codes(v_codes[1], v_words, *v_spans[1])
-        load_w(0, 0)
         load_err(0, 0)
+        load_codes(v_codes[1], v_words, *v_spans[1])
+        load_err(0, 1)
         load_codes(a_raw[1], a_words, PASS, 2 * PASS)
         load_scales(a_scale_raw[1], a_scales, PASS)
+        load_w(0, 0)
         load_w(1, 0)
-        load_err(0, 1)
         load_w(2, 0)
         load_err(1, 0)
         load_w(0, 1)
-        load_w(1, 1)
         load_err(1, 1)
+        load_w(1, 1)
         load_w(2, 1)
         load_neg_w(0)
         load_codes(v_codes[2], v_words, *v_spans[2])
@@ -137,15 +138,26 @@ def tile_movement_pruning_scores_s12_kernel(
         def quantize(codes, scale, values):
             nc.vector.quantize_mx(out=codes.bitcast(FP8X4), scales=scale, in_=values)
 
+        def sort_err(g, h, s, copy):
+            err_sorted[g, h, s] = stage.tile([PARTS, 2, 256], F32, name="err_sorted", bufs=6)
+            copy(
+                out=err_sorted[g, h, s][:].rearrange("p j (u w) -> p j u w", u=2),
+                in_=err_raw[g, h][:].bitcast(F32)[:, :, 256 * s : 256 * (s + 1)].rearrange("p j (w u) -> p j u w", u=2),
+            )
+
+        def err_words(g, h, j, s, u):
+            if (g, h, s) in err_sorted:
+                return err_sorted[g, h, s][:, j, 128 * u : 128 * (u + 1)]
+            return err_raw[g, h][:].bitcast(F32)[:, j, 256 * s + u : 256 * (s + 1) : 2]
+
         def transpose_err(g, h):
-            words = err_raw[g, h][:].bitcast(F32)
             for s in range(P_PASSES):
                 bank = take_bank()
                 for j in range(2):
                     for u in range(2):
                         nc.tensor.transpose(
                             bank[:, 256 * u + 128 * j : 256 * u + 128 * (j + 1)],
-                            words[:, j, 256 * s + u : 256 * (s + 1) : 2],
+                            err_words(g, h, j, s, u),
                             ident[:],
                         )
                 dst = err_bf[g, s][:].bitcast(F32).rearrange("p (t q r u) -> p t q r u", t=4, r=8, u=2)
@@ -167,10 +179,7 @@ def tile_movement_pruning_scores_s12_kernel(
 
         def token_product(passes, operands, width, evacuate, codes, scale):
             slots = BANK // width
-            values = stage.tile([PARTS, 4 * WIDE], BF16, name="values", align_bytes=64)
-            staged = values
-            if slots < 4:
-                staged = stage.tile([PARTS, 4 * WIDE], BF16, name="pairs", align_bytes=64)
+            staged = stage.tile([PARTS, 4 * WIDE], BF16, name="pairs", align_bytes=64, bufs=5)
             for b in range(4 // slots):
                 bank = take_bank()
                 for e in range(slots):
@@ -190,13 +199,17 @@ def tile_movement_pruning_scores_s12_kernel(
                     bank[:].rearrange("p (e n) -> p n e", e=slots),
                 )
 
+            joined = [staged]
+
             def join_pairs():
+                values = stage.tile([PARTS, 4 * WIDE], BF16, name="values", align_bytes=64, bufs=2)
+                joined.append(values)
                 nc.vector.tensor_copy(
                     out=values[:].bitcast(I32).rearrange("p (n b) -> p n b", b=2),
                     in_=staged[:].bitcast(I32).rearrange("p (b n) -> p n b", b=2),
                 )
 
-            return join_pairs, lambda: quantize(codes, scale, values[:, : 4 * width])
+            return join_pairs, lambda: quantize(codes, scale, joined[-1][:, : 4 * width])
 
         def x_product(g, f0, width):
             span = max(i for i, (lo, hi) in enumerate(v_spans) if lo <= f0)
@@ -268,54 +281,60 @@ def tile_movement_pruning_scores_s12_kernel(
             nc.scalar.activation(out=mask[:], in_=scores[:], func=ACT.Sigmoid)
             nc.sync.dma_start(out=out_1[rows, cols], in_=mask[:])
 
+        def sort_all(g, h, copy):
+            for s in range(P_PASSES):
+                sort_err(g, h, s, copy)
+
+        def finish(products):
+            products[0][0]()
+            for (join, quant), (join_after, quant_after) in zip(products, products[1:]):
+                join_after()
+                quant()
+            products[-1][1]()
+
         deal_a_codes(0)
         deal_a_scales(0)
-        join, quant = x_product(0, 0, WIDE)
-        interleave_w(0, 0)()
-        join_b, quant_b = x_product(0, WIDE, WIDE)
+        sort_all(0, 0, nc.vector.tensor_copy)
+        x_early = [x_product(0, 0, WIDE)]
+        sort_all(0, 1, nc.vector.tensor_copy)
+        x_early.append(x_product(0, WIDE, WIDE))
+        join, quant = x_early[0]
         join()
         deal_a_codes(1)
         quant()
         deal_a_scales(1)
+        join, quant = x_early[1]
+        join()
         transpose_err(0, 0)
-        join, quant = x_product(1, 0, WIDE)
-        quant_w = interleave_w(1, 0)
-        join_b()
+        x_early.append(x_product(1, 0, WIDE))
+        quant_w = interleave_w(0, 0)
+        quant()
+        quant_w_b = interleave_w(1, 0)
         quant_w()
-        quant_b()
-        transpose_err(0, 1)
         quant_w = interleave_w(2, 0)
-        join()
+        quant_w_b()
+        transpose_err(0, 1)
+        quantize_err(0, 0)
         quant_w()
-        quant()
-        join, quant = x_product(1, WIDE, WIDE)
-        for s in range(P_PASSES):
-            quantize_err(0, s)
+        quantize_err(0, 1)
+        quantize_err(0, 2)
+        x_early.append(x_product(1, WIDE, WIDE))
         transpose_err(1, 0)
-        quant_w = interleave_w(0, 1)
-        join()
-        quant_w()
-        quant()
-        join, quant = d_product(0, 0)
+        finish(x_early[2:])
+        d_early = [d_product(0, 0)]
         transpose_err(1, 1)
-        interleave_w(1, 1)()
+        interleave_w(0, 1)()
         for s in range(P_PASSES):
             quantize_err(1, s)
-        join()
-        quant_first = quant
-        join, quant = d_product(0, WIDE)
-        join_b, quant_b = d_product(1, 0)
-        quant_w = interleave_w(2, 1)
-        quant_first()
-        join()
+        d_early.append(d_product(0, WIDE))
+        d_early.append(d_product(1, 0))
+        quant_w = interleave_w(1, 1)
+        quant_w_b = interleave_w(2, 1)
         quant_w()
-        quant()
-        join, quant = d_product(1, WIDE)
-        join_b()
-        quant_b()
+        quant_w_b()
+        d_early.append(d_product(1, WIDE))
         join_b, quant_b = d_product(0, 2 * WIDE)
-        join()
-        quant()
+        finish(d_early)
 
         def two_grads(first, second, join, quant):
             grad_tile(*first)

from contextlib import ExitStack

import concourse.mybir as mybir
from concourse.masks import make_identity

M, K, F, P, N = 1024, 2048, 1024, 1536, 1024
FLOPS = 2 * M * K * F + 2 * M * P * N + 2 * M * F * N

F32 = mybir.dt.float32
BF16 = mybir.dt.bfloat16
I32 = mybir.dt.int32
U32 = mybir.dt.uint32
U8 = mybir.dt.uint8
FP8X4 = mybir.dt.float8_e4m3fn_x4
FP4X4 = mybir.dt.float4_e2m1fn_x4
ACT = mybir.ActivationFunctionType
ALU = mybir.AluOpType

PARTS = 128
PASS = 512
BANK = 512
BANKS = 8
K_PASSES = K // PASS
P_PASSES = P // PASS
GROUPS = M // PASS
WIDE = 256
NARROW = 128
OUT_BUFS = 6


def tile_movement_pruning_scores_s12_kernel(
    tc, a_words, a_scales, v_words, v_scales, err, w_next, neg_w, out_0, out_1
):
    nc = tc.nc
    with ExitStack() as ctx:
        keep = ctx.enter_context(tc.tile_pool(name="keep", bufs=1))
        stage = ctx.enter_context(tc.tile_pool(name="stage", bufs=3))
        outs = ctx.enter_context(tc.tile_pool(name="outs", bufs=OUT_BUFS))
        psum = ctx.enter_context(tc.psum_pool(name="psum", bufs=1))
        ctx.enter_context(tc.manual_schedule())

        def kept(name, shape, dtype):
            return keep.tile(shape, dtype, name=name, align_bytes=64)

        err_sorted = {}
        banks_taken = []

        def take_bank():
            name = "bank%d" % (len(banks_taken) % BANKS)
            banks_taken.append(name)
            return psum.tile([PARTS, BANK], F32, name=name)

        a_raw = [kept("a_raw%d" % g, [PARTS, K_PASSES, 2 * PASS], U8) for g in range(GROUPS)]
        a_codes = [kept("a_codes%d" % g, [PARTS, K_PASSES, 2 * PASS], U8) for g in range(GROUPS)]
        a_scale_raw = [kept("a_scale_raw%d" % g, [PARTS, K_PASSES, PASS], U8) for g in range(GROUPS)]
        a_scale = [kept("a_scale%d" % g, [PARTS, K_PASSES, PASS], U8) for g in range(GROUPS)]
        v_spans = [(0, WIDE), (WIDE, 2 * WIDE), (2 * WIDE, F)]
        v_codes = [kept("v_codes%d" % lo, [PARTS, K_PASSES, 2 * (hi - lo)], U8) for lo, hi in v_spans]
        v_scale = [kept("v_scale%d" % h, [PARTS, K_PASSES, BANK], U8) for h in range(2)]
        err_raw = {(g, h): kept("err_raw%d%d" % (g, h), [PARTS, 2, P], BF16) for g in range(GROUPS) for h in range(2)}
        err_bf = {(g, s): kept("err_bf%d%d" % (g, s), [PARTS, 4 * PASS], BF16) for g in range(GROUPS) for s in range(P_PASSES)}
        err_codes = {key: kept("err_codes%d%d" % key, [PARTS, PASS], U32) for key in err_bf}
        err_scale = {key: kept("err_scale%d%d" % key, [PARTS, PASS], U8) for key in err_bf}
        w_raw = {(s, h): kept("w_raw%d%d" % (s, h), [PARTS, 4, BANK], BF16) for s in range(P_PASSES) for h in range(2)}
        w_codes = {key: kept("w_codes%d%d" % key, [PARTS, BANK], U32) for key in w_raw}
        w_scale = {key: kept("w_scale%d%d" % key, [PARTS, BANK], U8) for key in w_raw}
        x_codes = [kept("x_codes%d" % g, [PARTS, F], U32) for g in range(GROUPS)]
        x_scale = [kept("x_scale%d" % g, [PARTS, F], U8) for g in range(GROUPS)]
        d_codes = [kept("d_codes%d" % g, [PARTS, N], U32) for g in range(GROUPS)]
        d_scale = [kept("d_scale%d" % g, [PARTS, N], U8) for g in range(GROUPS)]
        neg_w_sb = [kept("neg_w%d" % h, [PARTS, 4, N], BF16) for h in range(2)]
        ident = kept("ident", [PARTS, PARTS], F32)

        for plane in (a_scale_raw[0], v_scale[0], a_scale_raw[1], v_scale[1]):
            nc.vector.memset(plane[:].bitcast(I32), 0)
        make_identity(nc, ident[:])
        warm = kept("warm", [PARTS, 8], F32)
        nc.scalar.activation(out=warm[:], in_=ident[:, 0:8], func=ACT.Sigmoid)

        def load_codes(tile, words, lo, hi):
            src = words.bitcast(I32).rearrange("s p w -> p s w")
            nc.sync.dma_start(out=tile[:].bitcast(I32), in_=src[:, :, lo // 2 : hi // 2])

        def load_scales(plane, rows, lo, residues=range(4)):
            src = rows.bitcast(I32).rearrange("s (quad r) w -> r quad s w", r=4)
            for r in residues:
                nc.sync.dma_start(
                    out=plane[r:PARTS:32, :, :].bitcast(I32), in_=src[r][:, :, lo // 4 : (lo + PASS) // 4]
                )

        def load_err(g, h):
            rows = err[PASS * g + 256 * h : PASS * g + 256 * (h + 1), :]
            nc.sync.dma_start(out=err_raw[g, h][:], in_=rows.rearrange("(j p) k -> p j k", p=PARTS))

        def load_w(s, h):
            rows = w_next[PASS * s : PASS * (s + 1), BANK * h : BANK * (h + 1)]
            nc.sync.dma_start(out=w_raw[s, h][:], in_=rows.rearrange("(p j) n -> p j n", j=4))

        def load_neg_w(h):
            rows = neg_w[PASS * h : PASS * (h + 1), :]
            nc.sync.dma_start(out=neg_w_sb[h][:], in_=rows.rearrange("(j p) n -> p j n", p=PARTS))

        load_codes(v_codes[0], v_words, *v_spans[0])
        load_scales(a_scale_raw[0], a_scales, 0, (0, 1))
        load_codes(a_raw[0], a_words, 0, PASS)
        load_scales(a_scale_raw[0], a_scales, 0, (2, 3))
        load_scales(v_scale[0], v_scales, 0)
        load_err(0, 0)
        load_codes(v_codes[1], v_words, *v_spans[1])
        load_err(0, 1)
        load_codes(a_raw[1], a_words, PASS, 2 * PASS)
        load_scales(a_scale_raw[1], a_scales, PASS)
        load_w(0, 0)
        load_w(1, 0)
        load_w(2, 0)
        load_err(1, 0)
        load_w(0, 1)
        load_err(1, 1)
        load_w(1, 1)
        load_w(2, 1)
        load_neg_w(0)
        load_codes(v_codes[2], v_words, *v_spans[2])
        load_scales(v_scale[1], v_scales, BANK)
        load_neg_w(1)

        def deal(dst, src, run):
            nc.vector.tensor_copy(
                out=dst[:].bitcast(I32).rearrange("p s (t q w) -> p s t q w", t=4, w=run),
                in_=src[:].bitcast(I32).rearrange("p s (q t w) -> p s t q w", t=4, w=run),
            )

        def deal_a_codes(g):
            deal(a_codes[g], a_raw[g], 4)

        def deal_a_scales(g):
            deal(a_scale[g], a_scale_raw[g], 2)

        def quantize(codes, scale, values):
            nc.vector.quantize_mx(out=codes.bitcast(FP8X4), scales=scale, in_=values)

        def sort_err(g, h, s, copy):
            err_sorted[g, h, s] = stage.tile([PARTS, 2, 256], F32, name="err_sorted", bufs=6)
            copy(
                out=err_sorted[g, h, s][:].rearrange("p j (u w) -> p j u w", u=2),
                in_=err_raw[g, h][:].bitcast(F32)[:, :, 256 * s : 256 * (s + 1)].rearrange("p j (w u) -> p j u w", u=2),
            )

        def err_words(g, h, j, s, u):
            if (g, h, s) in err_sorted:
                return err_sorted[g, h, s][:, j, 128 * u : 128 * (u + 1)]
            return err_raw[g, h][:].bitcast(F32)[:, j, 256 * s + u : 256 * (s + 1) : 2]

        def transpose_err(g, h):
            for s in range(P_PASSES):
                bank = take_bank()
                for j in range(2):
                    for u in range(2):
                        nc.tensor.transpose(
                            bank[:, 256 * u + 128 * j : 256 * u + 128 * (j + 1)],
                            err_words(g, h, j, s, u),
                            ident[:],
                        )
                dst = err_bf[g, s][:].bitcast(F32).rearrange("p (t q r u) -> p t q r u", t=4, r=8, u=2)
                nc.scalar.copy(
                    out=dst[:, :, 8 * h : 8 * (h + 1), :, :],
                    in_=bank[:].rearrange("p (u q t r) -> p t q r u", u=2, t=4, r=8),
                )

        def quantize_err(g, s):
            quantize(err_codes[g, s][:], err_scale[g, s][:], err_bf[g, s][:])

        def interleave_w(s, h):
            w_bf = stage.tile([PARTS, 4 * BANK], BF16, name="w_bf", align_bytes=64)
            nc.vector.tensor_copy(
                out=w_bf[:].rearrange("p (c i j) -> p c j i", i=4, j=4),
                in_=w_raw[s, h][:].rearrange("p j (c i) -> p c j i", i=4),
            )
            return lambda: quantize(w_codes[s, h][:], w_scale[s, h][:], w_bf[:])

        def token_product(passes, operands, width, evacuate, codes, scale):
            slots = BANK // width
            staged = stage.tile([PARTS, 4 * WIDE], BF16, name="pairs", align_bytes=64, bufs=5)
            for b in range(4 // slots):
                bank = take_bank()
                for e in range(slots):
                    for s in range(passes):
                        lhs, lhs_scale, rhs, rhs_scale = operands(s, slots * b + e)
                        nc.tensor.matmul_mx(
                            out=bank[:, width * e : width * (e + 1)],
                            lhsT=lhs,
                            lhsT_scale=lhs_scale,
                            rhs=rhs,
                            rhs_scale=rhs_scale,
                            start=(s == 0),
                            stop=(s == passes - 1),
                        )
                evacuate(
                    staged[:, BANK * b : BANK * (b + 1)].rearrange("p (n e) -> p n e", e=slots),
                    bank[:].rearrange("p (e n) -> p n e", e=slots),
                )

            joined = [staged]

            def join_pairs():
                values = stage.tile([PARTS, 4 * WIDE], BF16, name="values", align_bytes=64, bufs=2)
                joined.append(values)
                nc.vector.tensor_copy(
                    out=values[:].bitcast(I32).rearrange("p (n b) -> p n b", b=2),
                    in_=staged[:].bitcast(I32).rearrange("p (b n) -> p n b", b=2),
                )

            return join_pairs, lambda: quantize(codes, scale, joined[-1][:, : 4 * width])

        def x_product(g, f0, width):
            span = max(i for i, (lo, hi) in enumerate(v_spans) if lo <= f0)
            c0 = f0 - v_spans[span][0]
            h, s0 = divmod(f0, BANK)

            def operands(s, t):
                return (
                    a_codes[g][:, s, 256 * t : 256 * (t + 1)].bitcast(FP4X4),
                    a_scale[g][:, s, 128 * t : 128 * (t + 1)],
                    v_codes[span][:, s, 2 * c0 : 2 * (c0 + width)].bitcast(FP4X4),
                    v_scale[h][:, s, s0 : s0 + width],
                )

            def evacuate(dst, src):
                if width == NARROW:
                    nc.vector.tensor_scalar(out=dst, in0=src, scalar1=0.0, scalar2=None, op0=ALU.max)
                else:
                    nc.scalar.activation(out=dst, in_=src, func=ACT.Relu)

            cols = slice(f0, f0 + width)
            return token_product(K_PASSES, operands, width, evacuate, x_codes[g][:, cols], x_scale[g][:, cols])

        def d_product(g, n0):
            h, c0 = divmod(n0, BANK)

            def operands(s, t):
                return (
                    err_codes[g, s][:, 128 * t : 128 * (t + 1)].bitcast(FP8X4),
                    err_scale[g, s][:, 128 * t : 128 * (t + 1)],
                    w_codes[s, h][:, c0 : c0 + WIDE].bitcast(FP8X4),
                    w_scale[s, h][:, c0 : c0 + WIDE],
                )

            def evacuate(dst, src):
                nc.scalar.copy(out=dst, in_=src)

            cols = slice(n0, n0 + WIDE)
            return token_product(P_PASSES, operands, WIDE, evacuate, d_codes[g][:, cols], d_scale[g][:, cols])

        def grad_pass(ft, h, g, bank):
            rows = slice(PARTS * ft, PARTS * (ft + 1))
            cols = slice(BANK * h, BANK * (h + 1))
            nc.tensor.matmul_mx(
                out=bank[:],
                lhsT=x_codes[g][:, rows].bitcast(FP8X4),
                lhsT_scale=x_scale[g][:, rows],
                rhs=d_codes[g][:, cols].bitcast(FP8X4),
                rhs_scale=d_scale[g][:, cols],
                start=(g == 0),
                stop=(g == GROUPS - 1),
            )

        def open_grad(ft, h):
            bank = take_bank()
            grad_pass(ft, h, 0, bank)
            return bank

        def grad_tile(ft, h, bank=None):
            rows = slice(PARTS * ft, PARTS * (ft + 1))
            cols = slice(BANK * h, BANK * (h + 1))
            if bank is None:
                bank = open_grad(ft, h)
            grad_pass(ft, h, 1, bank)
            scores = outs.tile([PARTS, BANK], F32, name="scores")
            nc.vector.tensor_tensor(out=scores[:], in0=bank[:], in1=neg_w_sb[ft // 4][:, ft % 4, cols], op=ALU.mult)
            nc.sync.dma_start(out=out_0[rows, cols], in_=scores[:])
            mask = outs.tile([PARTS, BANK], F32, name="mask")
            nc.scalar.activation(out=mask[:], in_=scores[:], func=ACT.Sigmoid)
            nc.sync.dma_start(out=out_1[rows, cols], in_=mask[:])

        def sort_all(g, h, copy):
            for s in range(P_PASSES):
                sort_err(g, h, s, copy)

        def finish(products):
            products[0][0]()
            for (join, quant), (join_after, quant_after) in zip(products, products[1:]):
                join_after()
                quant()
            products[-1][1]()

        deal_a_codes(0)
        deal_a_scales(0)
        sort_all(0, 0, nc.vector.tensor_copy)
        x_early = [x_product(0, 0, WIDE)]
        sort_all(0, 1, nc.vector.tensor_copy)
        x_early.append(x_product(0, WIDE, WIDE))
        join, quant = x_early[0]
        join()
        deal_a_codes(1)
        quant()
        deal_a_scales(1)
        join, quant = x_early[1]
        join()
        transpose_err(0, 0)
        x_early.append(x_product(1, 0, WIDE))
        quant_w = interleave_w(0, 0)
        quant()
        quant_w_b = interleave_w(1, 0)
        quant_w()
        quant_w = interleave_w(2, 0)
        quant_w_b()
        transpose_err(0, 1)
        quantize_err(0, 0)
        quant_w()
        quantize_err(0, 1)
        quantize_err(0, 2)
        x_early.append(x_product(1, WIDE, WIDE))
        transpose_err(1, 0)
        finish(x_early[2:])
        d_early = [d_product(0, 0)]
        transpose_err(1, 1)
        interleave_w(0, 1)()
        for s in range(P_PASSES):
            quantize_err(1, s)
        d_early.append(d_product(0, WIDE))
        d_early.append(d_product(1, 0))
        quant_w = interleave_w(1, 1)
        quant_w_b = interleave_w(2, 1)
        quant_w()
        quant_w_b()
        d_early.append(d_product(1, WIDE))
        join_b, quant_b = d_product(0, 2 * WIDE)
        finish(d_early)

        def two_grads(first, second, join, quant):
            grad_tile(*first)
            join()
            grad_tile(*second)
            quant()

        join, quant = d_product(1, 2 * WIDE)
        two_grads((0, 0), (1, 0), join_b, quant_b)
        join_b, quant_b = d_product(0, 3 * WIDE)
        join()
        quant()
        join, quant = d_product(1, 3 * WIDE)
        join_b()
        quant_b()
        join()
        grad_tile(2, 0)
        quant()
        grad_tile(3, 0)
        join, quant = x_product(0, 2 * WIDE, WIDE)
        two_grads((0, 1), (1, 1), join, quant)
        join, quant = x_product(1, 2 * WIDE, WIDE)
        join()
        grad_tile(2, 1)
        quant()
        grad_tile(3, 1)
        quant = x_product(0, 6 * NARROW, NARROW)[1]
        grad_tile(4, 0)
        quant()
        quant = x_product(1, 6 * NARROW, NARROW)[1]
        grad_tile(4, 1)
        quant()
        grad_tile(5, 0)
        quant = x_product(0, 7 * NARROW, NARROW)[1]
        grad_tile(5, 1)
        quant()
        grad_tile(6, 0)
        quant = x_product(1, 7 * NARROW, NARROW)[1]
        quant()
        grad_tile(6, 1)
        opened = [open_grad(7, h) for h in range(2)]
        for h in range(2):
            grad_tile(7, h, opened[h])
